import numpy as np
import ml_dtypes

BF16 = ml_dtypes.bfloat16


def bf(x):
    return np.asarray(x, np.float32).astype(BF16)


def f32(x):
    return np.asarray(x, np.float32)


def f64(x):
    return np.asarray(x).astype(np.float64)


def striped(idx):
    return np.tile(idx.reshape(-1, 16).T, (8, 1))


S, K, M, N, D, V = 2048, 128, 256, 2048, 4, 512


def setup_inputs():
    return {"table": bf(np.random.standard_normal((K, S))), "w": bf(np.random.standard_normal((D, K, M)) / np.sqrt(D * K)), "c": f32(0.2 + 0.8 * np.random.random_sample((1, V))), "offs": striped(np.random.permutation(np.tile(np.arange(S), 2))[:N])}


def reference(table, w, c, offs):
    idx = offs[:16].T.reshape(-1)
    x = f64(table)[:, idx]
    y = sum(f64(w)[t].T @ x[:, t * V : (t + 1) * V] for t in range(D))
    return y * f64(c)

@@ -1,0 +1,42 @@
+import concourse.mybir as mybir
+
+RELATIONS = 4
+FEATURES = 128
+NODES = 2048
+OUT_FEATURES = 256
+OUT_NODES = 512
+BLOCK = 128
+LANES = 16
+
+FLOPS = 2 * RELATIONS * FEATURES * OUT_FEATURES * OUT_NODES
+
+BF16, F32, U16 = mybir.dt.bfloat16, mybir.dt.float32, mybir.dt.uint16
+
+
+def tile_gather_matmul_kernel(tc, table, w, c, offs, out):
+    nc = tc.nc
+    columns = OUT_NODES // LANES
+    with (
+        tc.tile_pool(name="held", bufs=1) as held,
+        tc.psum_pool(name="psum", bufs=1) as psum,
+    ):
+        offsets = held.tile([128, RELATIONS * columns], U16, name="offsets")
+        nodes = held.tile([FEATURES, NODES], BF16, name="nodes")
+        weights = held.tile([FEATURES, RELATIONS, OUT_FEATURES], BF16, name="weights")
+        norm = held.tile([BLOCK, OUT_NODES], F32, name="norm")
+
+        nc.sync.dma_start(offsets[:], offs)
+        nc.sync.dma_start(nodes[:], table)
+        nc.scalar.dma_start(weights[:], w.rearrange("t k m -> k t m"))
+        nc.scalar.dma_start(norm[:], c[0, :].partition_broadcast(BLOCK))
+
+        for b in range(OUT_FEATURES // BLOCK):
+            rows = slice(b * BLOCK, (b + 1) * BLOCK)
+            bank = psum.tile([BLOCK, OUT_NODES], F32, name=f"bank{b}")
+            for t in range(RELATIONS):
+                picked = nodes[:].indirect(offsets[:, t * columns : (t + 1) * columns])
+                nc.tensor.matmul(bank[:], weights[:, t, rows], picked, start=(t == 0), stop=(t == RELATIONS - 1))
+
+            scaled = held.tile([BLOCK, OUT_NODES], F32, name=f"scaled{b}")
+            nc.vector.tensor_tensor(scaled[:], bank[:], norm[:], mybir.AluOpType.mult)
+            nc.sync.dma_start(out[rows, :], scaled[:])

@@ -15,12 +15,11 @@ BF16, F32, U16 = mybir.dt.bfloat16, mybir.dt.float32, mybir.dt.uint16
 
 def tile_gather_matmul_kernel(tc, table, w, c, offs, out):
     nc = tc.nc
-    columns = OUT_NODES // LANES
     with (
         tc.tile_pool(name="held", bufs=1) as held,
         tc.psum_pool(name="psum", bufs=1) as psum,
     ):
-        offsets = held.tile([128, RELATIONS * columns], U16, name="offsets")
+        offsets = held.tile([128, RELATIONS * OUT_NODES // LANES], U16, name="offsets")
         nodes = held.tile([FEATURES, NODES], BF16, name="nodes")
         weights = held.tile([FEATURES, RELATIONS, OUT_FEATURES], BF16, name="weights")
         norm = held.tile([BLOCK, OUT_NODES], F32, name="norm")
@@ -30,13 +29,19 @@ def tile_gather_matmul_kernel(tc, table, w, c, offs, out):
         nc.scalar.dma_start(weights[:], w.rearrange("t k m -> k t m"))
         nc.scalar.dma_start(norm[:], c[0, :].partition_broadcast(BLOCK))
 
-        for b in range(OUT_FEATURES // BLOCK):
+        blocks = OUT_FEATURES // BLOCK
+        for b in range(blocks):
             rows = slice(b * BLOCK, (b + 1) * BLOCK)
-            bank = psum.tile([BLOCK, OUT_NODES], F32, name=f"bank{b}")
-            for t in range(RELATIONS):
-                picked = nodes[:].indirect(offsets[:, t * columns : (t + 1) * columns])
-                nc.tensor.matmul(bank[:], weights[:, t, rows], picked, start=(t == 0), stop=(t == RELATIONS - 1))
+            parts = 2 if b == blocks - 1 else 1
+            width = OUT_NODES // parts
+            for h in range(parts):
+                cols = slice(h * width, (h + 1) * width)
+                bank = psum.tile([BLOCK, width], F32, name=f"bank{b}_{h}")
+                for t in range(RELATIONS):
+                    first = (t * OUT_NODES + h * width) // LANES
+                    picked = nodes[:].indirect(offsets[:, first : first + width // LANES])
+                    nc.tensor.matmul(bank[:], weights[:, t, rows], picked, start=(t == 0), stop=(t == RELATIONS - 1))
 
-            scaled = held.tile([BLOCK, OUT_NODES], F32, name=f"scaled{b}")
-            nc.vector.tensor_tensor(scaled[:], bank[:], norm[:], mybir.AluOpType.mult)
-            nc.sync.dma_start(out[rows, :], scaled[:])
+                scaled = held.tile([BLOCK, width], F32, name=f"scaled{b}_{h}")
+                nc.vector.tensor_tensor(scaled[:], bank[:], norm[:, cols], mybir.AluOpType.mult)
+                nc.sync.dma_start(out[rows, cols], scaled[:])

@@ -24,9 +24,9 @@ def tile_gather_matmul_kernel(tc, table, w, c, offs, out):
         weights = held.tile([FEATURES, RELATIONS, OUT_FEATURES], BF16, name="weights")
         norm = held.tile([BLOCK, OUT_NODES], F32, name="norm")
 
+        nc.scalar.dma_start(nodes[:], table)
         nc.sync.dma_start(offsets[:], offs)
-        nc.sync.dma_start(nodes[:], table)
-        nc.scalar.dma_start(weights[:], w.rearrange("t k m -> k t m"))
+        nc.sync.dma_start(weights[:], w.rearrange("t k m -> k t m"))
         nc.scalar.dma_start(norm[:], c[0, :].partition_broadcast(BLOCK))
 
         blocks = OUT_FEATURES // BLOCK

@@ -24,9 +24,11 @@ def tile_gather_matmul_kernel(tc, table, w, c, offs, out):
         weights = held.tile([FEATURES, RELATIONS, OUT_FEATURES], BF16, name="weights")
         norm = held.tile([BLOCK, OUT_NODES], F32, name="norm")
 
+        w_by_feature = w.rearrange("t k m -> k t m")
         nc.scalar.dma_start(nodes[:], table)
         nc.sync.dma_start(offsets[:], offs)
-        nc.sync.dma_start(weights[:], w.rearrange("t k m -> k t m"))
+        nc.sync.dma_start(weights[:, 0:1, :], w_by_feature[:, 0:1, :])
+        nc.scalar.dma_start(weights[:, 1:RELATIONS, :], w_by_feature[:, 1:RELATIONS, :])
         nc.scalar.dma_start(norm[:], c[0, :].partition_broadcast(BLOCK))
 
         blocks = OUT_FEATURES // BLOCK

import concourse.mybir as mybir

RELATIONS = 4
FEATURES = 128
NODES = 2048
OUT_FEATURES = 256
OUT_NODES = 512
BLOCK = 128
LANES = 16

FLOPS = 2 * RELATIONS * FEATURES * OUT_FEATURES * OUT_NODES

BF16, F32, U16 = mybir.dt.bfloat16, mybir.dt.float32, mybir.dt.uint16


def tile_gather_matmul_kernel(tc, table, w, c, offs, out):
    nc = tc.nc
    with (
        tc.tile_pool(name="held", bufs=1) as held,
        tc.psum_pool(name="psum", bufs=1) as psum,
    ):
        offsets = held.tile([128, RELATIONS * OUT_NODES // LANES], U16, name="offsets")
        nodes = held.tile([FEATURES, NODES], BF16, name="nodes")
        weights = held.tile([FEATURES, RELATIONS, OUT_FEATURES], BF16, name="weights")
        norm = held.tile([BLOCK, OUT_NODES], F32, name="norm")

        w_by_feature = w.rearrange("t k m -> k t m")
        nc.scalar.dma_start(nodes[:], table)
        nc.sync.dma_start(offsets[:], offs)
        nc.sync.dma_start(weights[:, 0:1, :], w_by_feature[:, 0:1, :])
        nc.scalar.dma_start(weights[:, 1:RELATIONS, :], w_by_feature[:, 1:RELATIONS, :])
        nc.scalar.dma_start(norm[:], c[0, :].partition_broadcast(BLOCK))

        blocks = OUT_FEATURES // BLOCK
        for b in range(blocks):
            rows = slice(b * BLOCK, (b + 1) * BLOCK)
            parts = 2 if b == blocks - 1 else 1
            width = OUT_NODES // parts
            for h in range(parts):
                cols = slice(h * width, (h + 1) * width)
                bank = psum.tile([BLOCK, width], F32, name=f"bank{b}_{h}")
                for t in range(RELATIONS):
                    first = (t * OUT_NODES + h * width) // LANES
                    picked = nodes[:].indirect(offsets[:, first : first + width // LANES])
                    nc.tensor.matmul(bank[:], weights[:, t, rows], picked, start=(t == 0), stop=(t == RELATIONS - 1))

                scaled = held.tile([BLOCK, width], F32, name=f"scaled{b}_{h}")
                nc.vector.tensor_tensor(scaled[:], bank[:], norm[:, cols], mybir.AluOpType.mult)
                nc.sync.dma_start(out[rows, cols], scaled[:])
